import numpy as np
import ml_dtypes


def mxq(x, axis, fmt="e4m3"):
    dtype, down = {"e4m3": (ml_dtypes.float8_e4m3fn, 7), "e5m2": (ml_dtypes.float8_e5m2, 14)}[fmt]
    v = np.moveaxis(np.asarray(x, np.float32).astype(ml_dtypes.bfloat16).astype(np.float64), axis, -1)
    blocks = v.reshape(v.shape[:-1] + (-1, 32))
    amax = np.abs(blocks).max(-1, keepdims=True)
    byte = np.maximum(np.where(amax > 0, np.frexp(amax)[1] - 1 + 127, 0) - down, 1)
    scale = np.exp2(byte - 127.0)
    codes = (blocks / scale).astype(np.float32).astype(dtype).astype(np.float64)
    return np.moveaxis((codes * scale).reshape(v.shape), -1, axis)


WIDE = False


def mx_kscale(k):
    if not WIDE:
        return np.ones(k)
    levels = np.array([30, -30])
    if k % 512:
        return np.exp2(np.random.permutation(np.resize(levels, k // 32))).repeat(32)
    a = np.empty((k // 512, 16))
    for p in range(k // 512):
        a[p, :8] = np.random.permutation(np.resize(levels, 8))
        for g in range(8):
            far = levels[np.abs(levels - a[p, g]) >= 10]
            a[p, g + 8] = far[np.random.randint(len(far))]
    return np.exp2(a.ravel()).repeat(32)


def f64(x):
    return np.asarray(x).astype(np.float64)


def striped(idx):
    return np.tile(np.asarray(idx).reshape(-1, 16).T, (8, 1)).astype(np.uint16)


def unstriped(offs):
    return offs[:16].T.reshape(-1).astype(np.int64)


E2M1 = np.array([0.0, 0.5, 1.0, 1.5, 2.0, 3.0, 4.0, 6.0, -0.0, -0.5, -1.0, -1.5, -2.0, -3.0, -4.0, -6.0])


def pack_weight(w, fmt):
    k, n = w.shape
    w = f64(np.asarray(w, np.float32).astype(ml_dtypes.bfloat16)).reshape(k // 32, 32, n)
    amax = np.abs(w).max(1)
    if fmt in ("e4m3", "e5m2"):
        byte = np.frexp(amax)[1] - 1 + 127 - (7 if fmt == "e4m3" else 14)
    else:
        mant, ex = np.frexp(amax / 6.0)
        byte = np.where(mant > 0.5, ex, ex - 1) + 127
    byte = np.clip(np.where(amax > 0, byte, 1), 1, 254)
    scaled = (w * np.exp2(127.0 - byte)[:, None, :]).reshape(k, n).astype(np.float32)
    by_word = np.ascontiguousarray(scaled.reshape(k // 512, 128, 4, n).transpose(0, 1, 3, 2))
    if fmt in ("e4m3", "e5m2"):
        words = by_word.astype(ml_dtypes.float8_e4m3fn if fmt == "e4m3" else ml_dtypes.float8_e5m2).view(np.uint8)
    else:
        c = by_word.astype(ml_dtypes.float4_e2m1fn).view(np.uint8) & 0xF
        words = (c[..., 0::2] | (c[..., 1::2] << 4)).reshape(k // 512, 128, 2 * n)
    return np.ascontiguousarray(words), np.ascontiguousarray(byte.astype(np.uint8).reshape(k // 512, 16, n))


def unpack_weight(words, scales, fmt):
    g, _, n = scales.shape
    words = np.ascontiguousarray(words).reshape(g, 128, n, -1)
    if fmt in ("e4m3", "e5m2"):
        vals = words.view(ml_dtypes.float8_e4m3fn if fmt == "e4m3" else ml_dtypes.float8_e5m2).astype(np.float64)
    else:
        nib = np.empty((g, 128, n, 4), np.uint8)
        nib[..., 0::2] = words & 0xF
        nib[..., 1::2] = words >> 4
        vals = E2M1[nib]
    vals = vals * np.repeat(np.exp2(scales.astype(np.float64) - 127.0), 8, axis=1)[..., None]
    return vals.transpose(0, 1, 3, 2).reshape(g * 512, n)


K, T, J, R, F, Z, N = 512, 512, 256, 512, 512, 1024, 256


def setup_inputs():
    n = np.random.standard_normal
    idx = np.random.permutation(T)[:J]
    idx2 = np.random.permutation(T)[:J]
    idx3 = np.random.permutation(Z)[:J]
    fk = mx_kscale(K)
    fr = mx_kscale(R)
    ff = mx_kscale(F)
    wp = pack_weight(n((K, R)) * 1 / np.sqrt(K) * fk[:, None] * fr, "e2m1")
    xop = pack_weight(n((F, Z)) / ff[:, None], "e4m3")
    w2p = pack_weight(n((F, R)) * 1 / np.sqrt(F) * ff[:, None] * fr, "e5m2")
    wbp = pack_weight(n((R, N)) * 1 / np.sqrt(R) / fr[:, None], "e5m2")
    return {
        "xf": (n((K, T))).astype(np.float32),
        "fk": (np.random.uniform(0.5, 2.0, (K, 1)) / fk[:, None]).astype(np.float32),
        "w_words": wp[0],
        "w_scales": wp[1],
        "xo_words": xop[0],
        "xo_scales": xop[1],
        "w2_words": w2p[0],
        "w2_scales": w2p[1],
        "wb_words": wbp[0],
        "wb_scales": wbp[1],
        "rs": (n((N, J))).astype(np.float32),
        "gm": (np.random.uniform(0.5, 2.0, (N, 1))).astype(np.float32),
        "offs": striped(idx),
        "offs2": striped(idx2),
        "offs3": striped(idx3),
    }


def reference(xf, fk, w_words, w_scales, xo_words, xo_scales, w2_words, w2_scales, wb_words, wb_scales, rs, gm, offs, offs2, offs3):
    idx = unstriped(offs)
    idx2 = unstriped(offs2)
    idx3 = unstriped(offs3)
    wu = unpack_weight(w_words, w_scales, "e2m1")
    xou = unpack_weight(xo_words, xo_scales, "e4m3")
    w2u = unpack_weight(w2_words, w2_scales, "e5m2")
    wbu = unpack_weight(wb_words, wb_scales, "e5m2")
    u = np.maximum(f64(xf)[:, idx], f64(xf)[:, idx2]) * f64(fk)
    uq = mxq(u, 0, "e4m3")
    a = wu.T @ uq
    xoidx3g = xou[:, idx3]
    q = w2u.T @ xoidx3g
    hid = np.abs(a - q)
    hidq = mxq(hid, 0, "e5m2")
    p = wbu.T @ hidq
    y = f64(gm) * p + f64(rs)
    return y

@@ -1,0 +1,218 @@
+from contextlib import ExitStack
+
+import concourse.mybir as mybir
+
+K, T, J, R, F, Z, N = 512, 512, 256, 512, 512, 1024, 256
+FLOPS = 2 * K * R * J + 2 * F * R * J + 2 * R * N * J
+
+F32 = mybir.dt.float32
+BF16 = mybir.dt.bfloat16
+I32 = mybir.dt.int32
+U32 = mybir.dt.uint32
+U16 = mybir.dt.uint16
+U8 = mybir.dt.uint8
+E4M3 = mybir.dt.float8_e4m3fn_x4
+E5M2 = mybir.dt.float8_e5m2_x4
+E2M1 = mybir.dt.float4_e2m1fn_x4
+ALU = mybir.AluOpType
+ACT = mybir.ActivationFunctionType
+
+P = 128
+PACK = 4
+HALF = 128
+HALVES = J // HALF
+LIST_COLS = HALF // 16
+
+
+def load_scale_rows(queue, plane, scales):
+    for quad in range(4):
+        queue.dma_start(
+            out=plane[32 * quad : 32 * quad + 4, :].bitcast(I32),
+            in_=scales[0, 4 * quad : 4 * quad + 4, :].bitcast(I32),
+        )
+
+
+def tile_list_two_largerpicks_other_absgap_residual_kernel(
+    tc, xf, fk, w_words, w_scales, xo_words, xo_scales, w2_words, w2_scales, wb_words, wb_scales, rs, gm, offs, offs2, offs3, out
+):
+    nc = tc.nc
+    with ExitStack() as ctx:
+        sb = ctx.enter_context(tc.tile_pool(name="sb", bufs=1))
+        ps = ctx.enter_context(tc.psum_pool(name="ps", bufs=1))
+
+        list_a = sb.tile([P, J // 16], U16, name="list_a")
+        list_b = sb.tile([P, J // 16], U16, name="list_b")
+        list_o = sb.tile([P, J // 16], U16, name="list_o")
+        x_plane = [sb.tile([P, T], F32, name="x_plane%d" % t) for t in range(PACK)]
+        fk_sb = sb.tile([P, PACK], F32, name="fk_sb")
+        fk_neg = sb.tile([P, PACK], F32, name="fk_neg")
+        gm_sb = sb.tile([P, N // P], F32, name="gm_sb")
+        rs_sb = sb.tile([P, N // P, J], F32, name="rs_sb")
+        w_raw = sb.tile([P, R], U16, name="w_raw")
+        w2_raw = sb.tile([P, R], U32, name="w2_raw")
+        ws_raw = sb.tile([P, 2 * R], U8, name="ws_raw")
+        xo_tab = sb.tile([P, Z], U32, name="xo_tab")
+        xo_tab_s = sb.tile([P, Z], U8, name="xo_tab_s")
+        wb_c = sb.tile([P, N], U32, name="wb_c", align_bytes=64)
+        wb_s = sb.tile([P, N], U8, name="wb_s", align_bytes=64)
+
+        nc.vector.memset(ws_raw[:].bitcast(I32), 0)
+        nc.vector.memset(xo_tab_s[:].bitcast(I32), 0)
+        nc.vector.memset(wb_s[:].bitcast(I32), 0)
+
+        x_rows = xf.rearrange("(p t) c -> p t c", t=PACK)
+        nc.sync.dma_start(list_a[:], offs)
+        nc.sync.dma_start(out=x_plane[0][:], in_=x_rows[:, 0, :])
+        nc.sync.dma_start(list_b[:], offs2)
+        nc.sync.dma_start(out=x_plane[1][:], in_=x_rows[:, 1, :])
+        nc.sync.dma_start(out=x_plane[2][:], in_=x_rows[:, 2, :])
+        nc.sync.dma_start(out=w2_raw[:].bitcast(I32), in_=w2_words[0].rearrange("p n t -> p (n t)").bitcast(I32))
+        nc.sync.dma_start(out=x_plane[3][:], in_=x_rows[:, 3, :])
+        nc.sync.dma_start(out=w_raw[:].bitcast(I32), in_=w_words[0].bitcast(I32))
+        nc.gpsimd.dma_start(out=fk_sb[:], in_=fk.rearrange("(p t) o -> p (t o)", t=PACK))
+        load_scale_rows(nc.gpsimd, ws_raw[:, 0:R], w_scales)
+        nc.sync.dma_start(list_o[:], offs3)
+        nc.sync.dma_start(out=xo_tab[:].bitcast(I32), in_=xo_words[0].rearrange("p n t -> p (n t)").bitcast(I32))
+        load_scale_rows(nc.sync, ws_raw[:, R : 2 * R], w2_scales)
+        load_scale_rows(nc.sync, xo_tab_s[:], xo_scales)
+        nc.sync.dma_start(out=wb_c[:].bitcast(I32), in_=wb_words[0].rearrange("p n t -> p (n t)").bitcast(I32))
+        load_scale_rows(nc.sync, wb_s[:], wb_scales)
+        with nc.allow_non_contiguous_dma(reason="one factor a partition and output tile"):
+            nc.sync.dma_start(out=gm_sb[:], in_=gm.rearrange("(c p) o -> p (c o)", p=P))
+        nc.sync.dma_start(out=rs_sb[:], in_=rs.rearrange("(c p) j -> p c j", p=P))
+
+        pick_a = sb.tile([P, PACK, J], F32, name="pick_a")
+        pick_b = sb.tile([P, PACK, J], F32, name="pick_b")
+        larger = sb.tile([P, PACK, J], F32, name="larger")
+
+        w_c = sb.tile([P, R], U16, name="w_c", align_bytes=64)
+        w2_c = sb.tile([P, R], U32, name="w2_c", align_bytes=64)
+        ws = sb.tile([P, 2 * R], U8, name="ws", align_bytes=64)
+        xo_c = sb.tile([P, J], U32, name="xo_c", align_bytes=64)
+        xo_s = sb.tile([P, J], U8, name="xo_s", align_bytes=64)
+        gap = [ps.tile([P, PACK, HALF], F32, name="gap%d" % h) for h in range(HALVES)]
+        prod = [ps.tile([P, N // P, HALF], F32, name="prod%d" % h) for h in range(HALVES)]
+        u_bf = [sb.tile([P, HALF * PACK], BF16, name="u_bf%d" % h, align_bytes=64) for h in range(HALVES)]
+        u_c = [sb.tile([P, HALF], U32, name="u_c%d" % h, align_bytes=64) for h in range(HALVES)]
+        u_s = [sb.tile([P, HALF], U8, name="u_s%d" % h, align_bytes=64) for h in range(HALVES)]
+        hid_bf = [sb.tile([P, HALF * PACK], BF16, name="hid_bf%d" % h, align_bytes=64) for h in range(HALVES)]
+        hid_c = [sb.tile([P, HALF], U32, name="hid_c%d" % h, align_bytes=64) for h in range(HALVES)]
+        hid_s = [sb.tile([P, HALF], U8, name="hid_s%d" % h, align_bytes=64) for h in range(HALVES)]
+        y = [sb.tile([P, N // P, HALF], F32, name="y%d" % h) for h in range(HALVES)]
+        out_rows = out.rearrange("(c p) j -> p c j", p=P)
+
+        def pick_scalar(dst, lst, t, lo, hi):
+            nc.scalar.activation(dst[:, t, lo:hi], x_plane[t][:].indirect(lst[:, lo // 16 : hi // 16]), ACT.Copy)
+
+        def pick_vector(dst, lst, t, lo, hi):
+            nc.vector.tensor_copy(dst[:, t, lo:hi], x_plane[t][:].indirect(lst[:, lo // 16 : hi // 16]))
+
+        def keep_larger(t0, t1, lo, hi):
+            nc.vector.tensor_tensor(larger[:, t0:t1, lo:hi], pick_a[:, t0:t1, lo:hi], pick_b[:, t0:t1, lo:hi], ALU.max)
+
+        def deal(dst, src):
+            nc.vector.tensor_copy(
+                out=dst.rearrange("p (t m) -> p m t", t=PACK), in_=src.rearrange("p (m t) -> p m t", t=PACK)
+            )
+
+        def scale_u(h):
+            nc.vector.tensor_tensor(
+                u_bf[h][:].rearrange("p (c i t) -> p c t i", i=4, t=PACK),
+                larger[:, :, h * HALF : (h + 1) * HALF].rearrange("p t (c i) -> p c t i", i=4),
+                fk_neg[:].unsqueeze(1).unsqueeze(3).to_broadcast([P, HALF // 4, PACK, 4]),
+                ALU.mult,
+            )
+
+        def quantize_u(h):
+            nc.vector.quantize_mx(out=u_c[h][:].bitcast(E4M3), scales=u_s[h][:], in_=u_bf[h][:])
+
+        def pick_side(h):
+            cols = slice(h * HALF, (h + 1) * HALF)
+            entries = list_o[:, h * LIST_COLS : (h + 1) * LIST_COLS]
+            nc.vector.tensor_copy(xo_c[:, cols], xo_tab[:].indirect(entries))
+            nc.vector.tensor_copy(xo_s[:, cols], xo_tab_s[:].indirect(entries))
+
+        def side_passes(h, first):
+            cols = slice(h * HALF, (h + 1) * HALF)
+            for t in range(PACK):
+                nc.tensor.matmul_mx(
+                    out=gap[h][:, t, :],
+                    lhsT=w2_c[:, t * P : (t + 1) * P].bitcast(E5M2),
+                    lhsT_scale=ws[:, R + t * P : R + (t + 1) * P],
+                    rhs=xo_c[:, cols].bitcast(E4M3),
+                    rhs_scale=xo_s[:, cols],
+                    start=(first and t == 0),
+                    stop=(not first and t == PACK - 1),
+                )
+
+        def token_passes(h, first):
+            for t in range(PACK):
+                nc.tensor.matmul_mx(
+                    out=gap[h][:, t, :],
+                    lhsT=w_c[:, t * P : (t + 1) * P].bitcast(E2M1),
+                    lhsT_scale=ws[:, t * P : (t + 1) * P],
+                    rhs=u_c[h][:].bitcast(E4M3),
+                    rhs_scale=u_s[h][:],
+                    start=(first and t == 0),
+                    stop=(not first and t == PACK - 1),
+                )
+
+        def magnitude(h):
+            nc.scalar.activation(
+                hid_bf[h][:].rearrange("p (j t) -> p j t", t=PACK), gap[h][:].rearrange("p t j -> p j t"), ACT.Abs
+            )
+
+        def second_stage(h):
+            nc.vector.quantize_mx(out=hid_c[h][:].bitcast(E5M2), scales=hid_s[h][:], in_=hid_bf[h][:])
+            for c in range(N // P):
+                nc.tensor.matmul_mx(
+                    out=prod[h][:, c, :],
+                    lhsT=wb_c[:, c * P : (c + 1) * P].bitcast(E5M2),
+                    lhsT_scale=wb_s[:, c * P : (c + 1) * P],
+                    rhs=hid_c[h][:].bitcast(E5M2),
+                    rhs_scale=hid_s[h][:],
+                    start=True,
+                    stop=True,
+                )
+
+        def finish(h):
+            cols = slice(h * HALF, (h + 1) * HALF)
+            for c in range(N // P):
+                nc.vector.scalar_tensor_tensor(
+                    y[h][:, c, :], prod[h][:, c, :], gm_sb[:, c : c + 1], rs_sb[:, c, cols], ALU.mult, ALU.add
+                )
+            nc.sync.dma_start(out=out_rows[:, :, cols], in_=y[h][:])
+
+        for t in range(2):
+            pick_scalar(pick_a, list_a, t, 0, J)
+            pick_vector(pick_b, list_b, t, 0, J)
+        pick_scalar(pick_a, list_a, 2, 0, J)
+        pick_scalar(pick_b, list_b, 2, 0, J)
+        for h in range(HALVES):
+            pick_scalar(pick_a, list_a, 3, h * HALF, (h + 1) * HALF)
+            pick_scalar(pick_b, list_b, 3, h * HALF, (h + 1) * HALF)
+        nc.vector.tensor_scalar(fk_neg[:], fk_sb[:], -1.0, None, ALU.mult)
+        keep_larger(0, 2, 0, J)
+        deal(w2_c[:], w2_raw[:])
+        keep_larger(2, 3, 0, J)
+        keep_larger(3, 4, 0, HALF)
+        deal(w_c[:], w_raw[:])
+        scale_u(0)
+        deal(ws[:, 0:R], ws_raw[:, 0:R])
+        quantize_u(0)
+        token_passes(0, True)
+        keep_larger(3, 4, HALF, J)
+        deal(ws[:, R : 2 * R], ws_raw[:, R : 2 * R])
+        pick_side(0)
+        side_passes(0, False)
+        magnitude(0)
+        scale_u(1)
+        pick_side(1)
+        side_passes(1, True)
+        quantize_u(1)
+        token_passes(1, False)
+        second_stage(0)
+        magnitude(1)
+        finish(0)
+        second_stage(1)
+        finish(1)

@@ -22,14 +22,9 @@ PACK = 4
 HALF = 128
 HALVES = J // HALF
 LIST_COLS = HALF // 16
-
-
-def load_scale_rows(queue, plane, scales):
-    for quad in range(4):
-        queue.dma_start(
-            out=plane[32 * quad : 32 * quad + 4, :].bitcast(I32),
-            in_=scales[0, 4 * quad : 4 * quad + 4, :].bitcast(I32),
-        )
+W_AT, W2_AT, XO_AT, WB_AT = 0, R, 2 * R, 2 * R + J
+SCALE_COLS = WB_AT + N
+ROWS_AT = P - 16
 
 
 def tile_list_two_largerpicks_other_absgap_residual_kernel(
@@ -43,43 +38,43 @@ def tile_list_two_largerpicks_other_absgap_residual_kernel(
         list_a = sb.tile([P, J // 16], U16, name="list_a")
         list_b = sb.tile([P, J // 16], U16, name="list_b")
         list_o = sb.tile([P, J // 16], U16, name="list_o")
-        x_plane = [sb.tile([P, T], F32, name="x_plane%d" % t) for t in range(PACK)]
+        x_first = sb.tile([P, T], F32, name="x_first")
+        x_rest = sb.tile([P, PACK - 1, T], F32, name="x_rest")
+        x_plane = [x_first[:]] + [x_rest[:, t, :] for t in range(PACK - 1)]
         fk_sb = sb.tile([P, PACK], F32, name="fk_sb")
         fk_neg = sb.tile([P, PACK], F32, name="fk_neg")
-        gm_sb = sb.tile([P, N // P], F32, name="gm_sb")
-        rs_sb = sb.tile([P, N // P, J], F32, name="rs_sb")
         w_raw = sb.tile([P, R], U16, name="w_raw")
         w2_raw = sb.tile([P, R], U32, name="w2_raw")
         ws_raw = sb.tile([P, 2 * R], U8, name="ws_raw")
         xo_tab = sb.tile([P, Z], U32, name="xo_tab")
         xo_tab_s = sb.tile([P, Z], U8, name="xo_tab_s")
+        rows = sb.tile([P, SCALE_COLS], U8, name="rows", tag="rows")
+        planes = sb.tile([P, SCALE_COLS], U8, name="planes", align_bytes=64)
         wb_c = sb.tile([P, N], U32, name="wb_c", align_bytes=64)
-        wb_s = sb.tile([P, N], U8, name="wb_s", align_bytes=64)
+        xo_picked_s = sb.tile([P, J], U8, name="xo_picked_s")
 
-        nc.vector.memset(ws_raw[:].bitcast(I32), 0)
-        nc.vector.memset(xo_tab_s[:].bitcast(I32), 0)
-        nc.vector.memset(wb_s[:].bitcast(I32), 0)
-
+        warm = sb.tile([P, 2], F32, name="warm")
+        nc.gpsimd.memset(warm[:, 0:1], 0.0)
+        nc.vector.memset(ws_raw[0:ROWS_AT, :].bitcast(I32), 0)
+        nc.vector.memset(xo_tab_s[0:ROWS_AT, :].bitcast(I32), 0)
+        nc.vector.memset(planes[:].bitcast(I32), 0)
         x_rows = xf.rearrange("(p t) c -> p t c", t=PACK)
         nc.sync.dma_start(list_a[:], offs)
-        nc.sync.dma_start(out=x_plane[0][:], in_=x_rows[:, 0, :])
-        nc.sync.dma_start(list_b[:], offs2)
-        nc.sync.dma_start(out=x_plane[1][:], in_=x_rows[:, 1, :])
-        nc.sync.dma_start(out=x_plane[2][:], in_=x_rows[:, 2, :])
-        nc.sync.dma_start(out=w2_raw[:].bitcast(I32), in_=w2_words[0].rearrange("p n t -> p (n t)").bitcast(I32))
-        nc.sync.dma_start(out=x_plane[3][:], in_=x_rows[:, 3, :])
-        nc.sync.dma_start(out=w_raw[:].bitcast(I32), in_=w_words[0].bitcast(I32))
-        nc.gpsimd.dma_start(out=fk_sb[:], in_=fk.rearrange("(p t) o -> p (t o)", t=PACK))
-        load_scale_rows(nc.gpsimd, ws_raw[:, 0:R], w_scales)
+        nc.scalar.dma_start(out=ws_raw[ROWS_AT:P, R : 2 * R].bitcast(I32), in_=w2_scales[0].bitcast(I32))
+        nc.scalar.dma_start(out=ws_raw[ROWS_AT:P, 0:R].bitcast(I32), in_=w_scales[0].bitcast(I32))
+        nc.scalar.dma_start(out=xo_tab_s[ROWS_AT:P, :].bitcast(I32), in_=xo_scales[0].bitcast(I32))
+        nc.sync.dma_start(out=x_first[:], in_=x_rows[:, 0, :])
         nc.sync.dma_start(list_o[:], offs3)
+        nc.sync.dma_start(list_b[:], offs2)
+        nc.sync.dma_start(out=x_rest[:], in_=x_rows[:, 1:PACK, :])
+        nc.scalar.activation(warm[:, 1:2], warm[:, 0:1], ACT.Copy)
+        nc.gpsimd.dma_start(out=fk_sb[:], in_=fk.rearrange("(p t) o -> p (t o)", t=PACK))
+        nc.gpsimd.tensor_scalar(fk_neg[:], fk_sb[:], -1.0, 0.0, ALU.mult, ALU.add)
+        nc.sync.dma_start(out=w2_raw[:].bitcast(I32), in_=w2_words[0].rearrange("p n t -> p (n t)").bitcast(I32))
+        nc.sync.dma_start(out=w_raw[:].bitcast(I32), in_=w_words[0].bitcast(I32))
         nc.sync.dma_start(out=xo_tab[:].bitcast(I32), in_=xo_words[0].rearrange("p n t -> p (n t)").bitcast(I32))
-        load_scale_rows(nc.sync, ws_raw[:, R : 2 * R], w2_scales)
-        load_scale_rows(nc.sync, xo_tab_s[:], xo_scales)
+        nc.sync.dma_start(out=rows[ROWS_AT:P, WB_AT:SCALE_COLS].bitcast(I32), in_=wb_scales[0].bitcast(I32))
         nc.sync.dma_start(out=wb_c[:].bitcast(I32), in_=wb_words[0].rearrange("p n t -> p (n t)").bitcast(I32))
-        load_scale_rows(nc.sync, wb_s[:], wb_scales)
-        with nc.allow_non_contiguous_dma(reason="one factor a partition and output tile"):
-            nc.sync.dma_start(out=gm_sb[:], in_=gm.rearrange("(c p) o -> p (c o)", p=P))
-        nc.sync.dma_start(out=rs_sb[:], in_=rs.rearrange("(c p) j -> p c j", p=P))
 
         pick_a = sb.tile([P, PACK, J], F32, name="pick_a")
         pick_b = sb.tile([P, PACK, J], F32, name="pick_b")
@@ -87,9 +82,7 @@ def tile_list_two_largerpicks_other_absgap_residual_kernel(
 
         w_c = sb.tile([P, R], U16, name="w_c", align_bytes=64)
         w2_c = sb.tile([P, R], U32, name="w2_c", align_bytes=64)
-        ws = sb.tile([P, 2 * R], U8, name="ws", align_bytes=64)
         xo_c = sb.tile([P, J], U32, name="xo_c", align_bytes=64)
-        xo_s = sb.tile([P, J], U8, name="xo_s", align_bytes=64)
         gap = [ps.tile([P, PACK, HALF], F32, name="gap%d" % h) for h in range(HALVES)]
         prod = [ps.tile([P, N // P, HALF], F32, name="prod%d" % h) for h in range(HALVES)]
         u_bf = [sb.tile([P, HALF * PACK], BF16, name="u_bf%d" % h, align_bytes=64) for h in range(HALVES)]
@@ -102,10 +95,10 @@ def tile_list_two_largerpicks_other_absgap_residual_kernel(
         out_rows = out.rearrange("(c p) j -> p c j", p=P)
 
         def pick_scalar(dst, lst, t, lo, hi):
-            nc.scalar.activation(dst[:, t, lo:hi], x_plane[t][:].indirect(lst[:, lo // 16 : hi // 16]), ACT.Copy)
+            nc.scalar.activation(dst[:, t, lo:hi], x_plane[t].indirect(lst[:, lo // 16 : hi // 16]), ACT.Copy)
 
         def pick_vector(dst, lst, t, lo, hi):
-            nc.vector.tensor_copy(dst[:, t, lo:hi], x_plane[t][:].indirect(lst[:, lo // 16 : hi // 16]))
+            nc.vector.tensor_copy(dst[:, t, lo:hi], x_plane[t].indirect(lst[:, lo // 16 : hi // 16]))
 
         def keep_larger(t0, t1, lo, hi):
             nc.vector.tensor_tensor(larger[:, t0:t1, lo:hi], pick_a[:, t0:t1, lo:hi], pick_b[:, t0:t1, lo:hi], ALU.max)
@@ -130,7 +123,6 @@ def tile_list_two_largerpicks_other_absgap_residual_kernel(
             cols = slice(h * HALF, (h + 1) * HALF)
             entries = list_o[:, h * LIST_COLS : (h + 1) * LIST_COLS]
             nc.vector.tensor_copy(xo_c[:, cols], xo_tab[:].indirect(entries))
-            nc.vector.tensor_copy(xo_s[:, cols], xo_tab_s[:].indirect(entries))
 
         def side_passes(h, first):
             cols = slice(h * HALF, (h + 1) * HALF)
@@ -138,9 +130,9 @@ def tile_list_two_largerpicks_other_absgap_residual_kernel(
                 nc.tensor.matmul_mx(
                     out=gap[h][:, t, :],
                     lhsT=w2_c[:, t * P : (t + 1) * P].bitcast(E5M2),
-                    lhsT_scale=ws[:, R + t * P : R + (t + 1) * P],
+                    lhsT_scale=planes[:, W2_AT + t * P : W2_AT + (t + 1) * P],
                     rhs=xo_c[:, cols].bitcast(E4M3),
-                    rhs_scale=xo_s[:, cols],
+                    rhs_scale=planes[:, XO_AT + h * HALF : XO_AT + (h + 1) * HALF],
                     start=(first and t == 0),
                     stop=(not first and t == PACK - 1),
                 )
@@ -150,7 +142,7 @@ def tile_list_two_largerpicks_other_absgap_residual_kernel(
                 nc.tensor.matmul_mx(
                     out=gap[h][:, t, :],
                     lhsT=w_c[:, t * P : (t + 1) * P].bitcast(E2M1),
-                    lhsT_scale=ws[:, t * P : (t + 1) * P],
+                    lhsT_scale=planes[:, W_AT + t * P : W_AT + (t + 1) * P],
                     rhs=u_c[h][:].bitcast(E4M3),
                     rhs_scale=u_s[h][:],
                     start=(first and t == 0),
@@ -168,7 +160,7 @@ def tile_list_two_largerpicks_other_absgap_residual_kernel(
                 nc.tensor.matmul_mx(
                     out=prod[h][:, c, :],
                     lhsT=wb_c[:, c * P : (c + 1) * P].bitcast(E5M2),
-                    lhsT_scale=wb_s[:, c * P : (c + 1) * P],
+                    lhsT_scale=planes[:, WB_AT + c * P : WB_AT + (c + 1) * P],
                     rhs=hid_c[h][:].bitcast(E5M2),
                     rhs_scale=hid_s[h][:],
                     start=True,
@@ -183,36 +175,50 @@ def tile_list_two_largerpicks_other_absgap_residual_kernel(
                 )
             nc.sync.dma_start(out=out_rows[:, :, cols], in_=y[h][:])
 
-        for t in range(2):
-            pick_scalar(pick_a, list_a, t, 0, J)
-            pick_vector(pick_b, list_b, t, 0, J)
+        nc.vector.tensor_copy(
+            out=rows[:, W_AT:XO_AT].rearrange("p (s t m) -> p s m t", s=2, t=PACK),
+            in_=ws_raw[:].rearrange("p (s m t) -> p s m t", s=2, t=PACK),
+        )
+        nc.vector.tensor_copy(xo_picked_s[:], xo_tab_s[:].indirect(list_o[:]))
+        nc.vector.tensor_copy(rows[:, XO_AT : XO_AT + J].bitcast(I32), xo_picked_s[:].bitcast(I32))
+        for quad in range(4):
+            nc.sync.dma_start(
+                out=planes[32 * quad : 32 * quad + 4, :].bitcast(I32), in_=rows[ROWS_AT + 4 * quad : ROWS_AT + 4 * quad + 4, :].bitcast(I32)
+            )
+        pick_scalar(pick_a, list_a, 0, 0, J)
+        pick_scalar(pick_b, list_b, 0, 0, J)
+        pick_scalar(pick_a, list_a, 1, 0, J)
+        pick_vector(pick_b, list_b, 1, 0, J)
         pick_scalar(pick_a, list_a, 2, 0, J)
         pick_scalar(pick_b, list_b, 2, 0, J)
         for h in range(HALVES):
             pick_scalar(pick_a, list_a, 3, h * HALF, (h + 1) * HALF)
             pick_scalar(pick_b, list_b, 3, h * HALF, (h + 1) * HALF)
-        nc.vector.tensor_scalar(fk_neg[:], fk_sb[:], -1.0, None, ALU.mult)
-        keep_larger(0, 2, 0, J)
+        late = sb.tile([P, (N // P) * (J + 1)], F32, name="late", tag="rows")
+        rs_sb = late[:, 0 : (N // P) * J].rearrange("p (c j) -> p c j", j=J)
+        gm_sb = late[:, (N // P) * J :]
+        nc.sync.dma_start(out=rs_sb, in_=rs.rearrange("(c p) j -> p c j", p=P))
+        with nc.allow_non_contiguous_dma(reason="one factor a partition and output tile"):
+            nc.sync.dma_start(out=gm_sb, in_=gm.rearrange("(c p) o -> p (c o)", p=P))
         deal(w2_c[:], w2_raw[:])
-        keep_larger(2, 3, 0, J)
-        keep_larger(3, 4, 0, HALF)
         deal(w_c[:], w_raw[:])
-        scale_u(0)
-        deal(ws[:, 0:R], ws_raw[:, 0:R])
-        quantize_u(0)
-        token_passes(0, True)
-        keep_larger(3, 4, HALF, J)
-        deal(ws[:, R : 2 * R], ws_raw[:, R : 2 * R])
+        keep_larger(0, 2, 0, J)
         pick_side(0)
-        side_passes(0, False)
-        magnitude(0)
-        scale_u(1)
+        side_passes(0, True)
         pick_side(1)
         side_passes(1, True)
+        keep_larger(2, 3, 0, J)
+        keep_larger(3, 4, 0, HALF)
+        scale_u(0)
+        keep_larger(3, 4, HALF, J)
+        quantize_u(0)
+        token_passes(0, False)
+        magnitude(0)
+        scale_u(1)
         quantize_u(1)
         token_passes(1, False)
         second_stage(0)
         magnitude(1)
-        finish(0)
         second_stage(1)
+        finish(0)
         finish(1)

@@ -38,20 +38,18 @@ def tile_list_two_largerpicks_other_absgap_residual_kernel(
         list_a = sb.tile([P, J // 16], U16, name="list_a")
         list_b = sb.tile([P, J // 16], U16, name="list_b")
         list_o = sb.tile([P, J // 16], U16, name="list_o")
-        x_first = sb.tile([P, T], F32, name="x_first")
-        x_rest = sb.tile([P, PACK - 1, T], F32, name="x_rest")
-        x_plane = [x_first[:]] + [x_rest[:, t, :] for t in range(PACK - 1)]
+        x_pair = [sb.tile([P, 2, T], F32, name="x_pair%d" % a) for a in range(2)]
+        x_plane = [x_pair[t // 2][:, t % 2, :] for t in range(PACK)]
         fk_sb = sb.tile([P, PACK], F32, name="fk_sb")
         fk_neg = sb.tile([P, PACK], F32, name="fk_neg")
-        w_raw = sb.tile([P, R], U16, name="w_raw")
-        w2_raw = sb.tile([P, R], U32, name="w2_raw")
+        w_raw = sb.tile([P, R], U16, name="w_raw", tag="w_raw", align_bytes=64)
+        w2_raw = sb.tile([P, R], U32, name="w2_raw", tag="w2_raw")
         ws_raw = sb.tile([P, 2 * R], U8, name="ws_raw")
-        xo_tab = sb.tile([P, Z], U32, name="xo_tab")
+        xo_tab = sb.tile([P, Z], U32, name="xo_tab", tag="xo_tab")
         xo_tab_s = sb.tile([P, Z], U8, name="xo_tab_s")
         rows = sb.tile([P, SCALE_COLS], U8, name="rows", tag="rows")
         planes = sb.tile([P, SCALE_COLS], U8, name="planes", align_bytes=64)
-        wb_c = sb.tile([P, N], U32, name="wb_c", align_bytes=64)
-        xo_picked_s = sb.tile([P, J], U8, name="xo_picked_s")
+        xo_picked_s = sb.tile([P, J], U8, name="xo_picked_s", tag="after_spread", align_bytes=64)
 
         warm = sb.tile([P, 2], F32, name="warm")
         nc.gpsimd.memset(warm[:, 0:1], 0.0)
@@ -59,33 +57,30 @@ def tile_list_two_largerpicks_other_absgap_residual_kernel(
         nc.vector.memset(xo_tab_s[0:ROWS_AT, :].bitcast(I32), 0)
         nc.vector.memset(planes[:].bitcast(I32), 0)
         x_rows = xf.rearrange("(p t) c -> p t c", t=PACK)
+        nc.sync.dma_start(list_o[:], offs3)
+        nc.scalar.dma_start(out=xo_tab_s[ROWS_AT:P, :].bitcast(I32), in_=xo_scales[0].bitcast(I32))
         nc.sync.dma_start(list_a[:], offs)
         nc.scalar.dma_start(out=ws_raw[ROWS_AT:P, R : 2 * R].bitcast(I32), in_=w2_scales[0].bitcast(I32))
         nc.scalar.dma_start(out=ws_raw[ROWS_AT:P, 0:R].bitcast(I32), in_=w_scales[0].bitcast(I32))
-        nc.scalar.dma_start(out=xo_tab_s[ROWS_AT:P, :].bitcast(I32), in_=xo_scales[0].bitcast(I32))
-        nc.sync.dma_start(out=x_first[:], in_=x_rows[:, 0, :])
-        nc.sync.dma_start(list_o[:], offs3)
+        nc.sync.dma_start(out=x_pair[0][:], in_=x_rows[:, 0:2, :])
         nc.sync.dma_start(list_b[:], offs2)
-        nc.sync.dma_start(out=x_rest[:], in_=x_rows[:, 1:PACK, :])
+        nc.sync.dma_start(out=x_pair[1][:], in_=x_rows[:, 2:4, :])
         nc.scalar.activation(warm[:, 1:2], warm[:, 0:1], ACT.Copy)
-        nc.gpsimd.dma_start(out=fk_sb[:], in_=fk.rearrange("(p t) o -> p (t o)", t=PACK))
+        nc.sync.dma_start(out=fk_sb[:], in_=fk.rearrange("(p t) o -> p (t o)", t=PACK))
         nc.gpsimd.tensor_scalar(fk_neg[:], fk_sb[:], -1.0, 0.0, ALU.mult, ALU.add)
+        nc.sync.dma_start(out=rows[ROWS_AT:P, WB_AT:SCALE_COLS].bitcast(I32), in_=wb_scales[0].bitcast(I32))
+        nc.sync.dma_start(out=xo_tab[:].bitcast(I32), in_=xo_words[0].rearrange("p n t -> p (n t)").bitcast(I32))
         nc.sync.dma_start(out=w2_raw[:].bitcast(I32), in_=w2_words[0].rearrange("p n t -> p (n t)").bitcast(I32))
         nc.sync.dma_start(out=w_raw[:].bitcast(I32), in_=w_words[0].bitcast(I32))
-        nc.sync.dma_start(out=xo_tab[:].bitcast(I32), in_=xo_words[0].rearrange("p n t -> p (n t)").bitcast(I32))
-        nc.sync.dma_start(out=rows[ROWS_AT:P, WB_AT:SCALE_COLS].bitcast(I32), in_=wb_scales[0].bitcast(I32))
-        nc.sync.dma_start(out=wb_c[:].bitcast(I32), in_=wb_words[0].rearrange("p n t -> p (n t)").bitcast(I32))
 
         pick_a = sb.tile([P, PACK, J], F32, name="pick_a")
         pick_b = sb.tile([P, PACK, J], F32, name="pick_b")
-        larger = sb.tile([P, PACK, J], F32, name="larger")
 
         w_c = sb.tile([P, R], U16, name="w_c", align_bytes=64)
         w2_c = sb.tile([P, R], U32, name="w2_c", align_bytes=64)
         xo_c = sb.tile([P, J], U32, name="xo_c", align_bytes=64)
         gap = [ps.tile([P, PACK, HALF], F32, name="gap%d" % h) for h in range(HALVES)]
         prod = [ps.tile([P, N // P, HALF], F32, name="prod%d" % h) for h in range(HALVES)]
-        u_bf = [sb.tile([P, HALF * PACK], BF16, name="u_bf%d" % h, align_bytes=64) for h in range(HALVES)]
         u_c = [sb.tile([P, HALF], U32, name="u_c%d" % h, align_bytes=64) for h in range(HALVES)]
         u_s = [sb.tile([P, HALF], U8, name="u_s%d" % h, align_bytes=64) for h in range(HALVES)]
         hid_bf = [sb.tile([P, HALF * PACK], BF16, name="hid_bf%d" % h, align_bytes=64) for h in range(HALVES)]
@@ -100,29 +95,26 @@ def tile_list_two_largerpicks_other_absgap_residual_kernel(
         def pick_vector(dst, lst, t, lo, hi):
             nc.vector.tensor_copy(dst[:, t, lo:hi], x_plane[t].indirect(lst[:, lo // 16 : hi // 16]))
 
-        def keep_larger(t0, t1, lo, hi):
-            nc.vector.tensor_tensor(larger[:, t0:t1, lo:hi], pick_a[:, t0:t1, lo:hi], pick_b[:, t0:t1, lo:hi], ALU.max)
+        def keep_larger(larger, h):
+            cols = slice(h * HALF, (h + 1) * HALF)
+            nc.vector.tensor_tensor(larger[:], pick_a[:, :, cols], pick_b[:, :, cols], ALU.max)
 
-        def deal(dst, src):
+        def deal(dst, src, per_line):
             nc.vector.tensor_copy(
-                out=dst.rearrange("p (t m) -> p m t", t=PACK), in_=src.rearrange("p (m t) -> p m t", t=PACK)
+                out=dst.rearrange("p (s t c i) -> p s c t i", t=PACK, c=P // per_line, i=per_line),
+                in_=src.rearrange("p (s c i t) -> p s c t i", t=PACK, c=P // per_line, i=per_line),
             )
 
-        def scale_u(h):
+        def scale_u(u_bf, larger):
             nc.vector.tensor_tensor(
-                u_bf[h][:].rearrange("p (c i t) -> p c t i", i=4, t=PACK),
-                larger[:, :, h * HALF : (h + 1) * HALF].rearrange("p t (c i) -> p c t i", i=4),
+                u_bf[:].rearrange("p (c i t) -> p c t i", i=4, t=PACK),
+                larger[:].rearrange("p t (c i) -> p c t i", i=4),
                 fk_neg[:].unsqueeze(1).unsqueeze(3).to_broadcast([P, HALF // 4, PACK, 4]),
                 ALU.mult,
             )
 
-        def quantize_u(h):
-            nc.vector.quantize_mx(out=u_c[h][:].bitcast(E4M3), scales=u_s[h][:], in_=u_bf[h][:])
-
-        def pick_side(h):
-            cols = slice(h * HALF, (h + 1) * HALF)
-            entries = list_o[:, h * LIST_COLS : (h + 1) * LIST_COLS]
-            nc.vector.tensor_copy(xo_c[:, cols], xo_tab[:].indirect(entries))
+        def quantize_u(u_bf, h):
+            nc.vector.quantize_mx(out=u_c[h][:].bitcast(E4M3), scales=u_s[h][:], in_=u_bf[:])
 
         def side_passes(h, first):
             cols = slice(h * HALF, (h + 1) * HALF)
@@ -173,49 +165,48 @@ def tile_list_two_largerpicks_other_absgap_residual_kernel(
                 nc.vector.scalar_tensor_tensor(
                     y[h][:, c, :], prod[h][:, c, :], gm_sb[:, c : c + 1], rs_sb[:, c, cols], ALU.mult, ALU.add
                 )
-            nc.sync.dma_start(out=out_rows[:, :, cols], in_=y[h][:])
+                nc.sync.dma_start(out=out_rows[:, c, cols], in_=y[h][:, c, :])
 
-        nc.vector.tensor_copy(
-            out=rows[:, W_AT:XO_AT].rearrange("p (s t m) -> p s m t", s=2, t=PACK),
-            in_=ws_raw[:].rearrange("p (s m t) -> p s m t", s=2, t=PACK),
-        )
         nc.vector.tensor_copy(xo_picked_s[:], xo_tab_s[:].indirect(list_o[:]))
+        deal(rows[:, W_AT:XO_AT], ws_raw[:], 16)
         nc.vector.tensor_copy(rows[:, XO_AT : XO_AT + J].bitcast(I32), xo_picked_s[:].bitcast(I32))
         for quad in range(4):
             nc.sync.dma_start(
                 out=planes[32 * quad : 32 * quad + 4, :].bitcast(I32), in_=rows[ROWS_AT + 4 * quad : ROWS_AT + 4 * quad + 4, :].bitcast(I32)
             )
+        wb_c = sb.tile([P, N], U32, name="wb_c", tag="after_spread", align_bytes=64)
+        nc.sync.dma_start(out=wb_c[:].bitcast(I32), in_=wb_words[0].rearrange("p n t -> p (n t)").bitcast(I32))
         pick_scalar(pick_a, list_a, 0, 0, J)
-        pick_scalar(pick_b, list_b, 0, 0, J)
+        pick_vector(pick_b, list_b, 0, 0, J)
         pick_scalar(pick_a, list_a, 1, 0, J)
         pick_vector(pick_b, list_b, 1, 0, J)
-        pick_scalar(pick_a, list_a, 2, 0, J)
-        pick_scalar(pick_b, list_b, 2, 0, J)
         for h in range(HALVES):
-            pick_scalar(pick_a, list_a, 3, h * HALF, (h + 1) * HALF)
-            pick_scalar(pick_b, list_b, 3, h * HALF, (h + 1) * HALF)
+            for t in range(2, PACK):
+                pick_scalar(pick_a, list_a, t, h * HALF, (h + 1) * HALF)
+                pick_scalar(pick_b, list_b, t, h * HALF, (h + 1) * HALF)
         late = sb.tile([P, (N // P) * (J + 1)], F32, name="late", tag="rows")
         rs_sb = late[:, 0 : (N // P) * J].rearrange("p (c j) -> p c j", j=J)
         gm_sb = late[:, (N // P) * J :]
         nc.sync.dma_start(out=rs_sb, in_=rs.rearrange("(c p) j -> p c j", p=P))
         with nc.allow_non_contiguous_dma(reason="one factor a partition and output tile"):
             nc.sync.dma_start(out=gm_sb, in_=gm.rearrange("(c p) o -> p (c o)", p=P))
-        deal(w2_c[:], w2_raw[:])
-        deal(w_c[:], w_raw[:])
-        keep_larger(0, 2, 0, J)
-        pick_side(0)
+        nc.vector.tensor_copy(xo_c[:], xo_tab[:].indirect(list_o[:]))
+        larger0 = sb.tile([P, PACK, HALF], F32, name="larger0", tag="xo_tab")
+        u_bf0 = sb.tile([P, HALF * PACK], BF16, name="u_bf0", align_bytes=64)
+        keep_larger(larger0, 0)
+        deal(w2_c[:], w2_raw[:], 4)
         side_passes(0, True)
-        pick_side(1)
         side_passes(1, True)
-        keep_larger(2, 3, 0, J)
-        keep_larger(3, 4, 0, HALF)
-        scale_u(0)
-        keep_larger(3, 4, HALF, J)
-        quantize_u(0)
+        scale_u(u_bf0, larger0)
+        deal(w_c[:], w_raw[:], 8)
+        quantize_u(u_bf0, 0)
         token_passes(0, False)
         magnitude(0)
-        scale_u(1)
-        quantize_u(1)
+        larger1 = sb.tile([P, PACK, HALF], F32, name="larger1", tag="w2_raw")
+        u_bf1 = sb.tile([P, HALF * PACK], BF16, name="u_bf1", tag="w_raw", align_bytes=64)
+        keep_larger(larger1, 1)
+        scale_u(u_bf1, larger1)
+        quantize_u(u_bf1, 1)
         token_passes(1, False)
         second_stage(0)
         magnitude(1)

from contextlib import ExitStack

import concourse.mybir as mybir

K, T, J, R, F, Z, N = 512, 512, 256, 512, 512, 1024, 256
FLOPS = 2 * K * R * J + 2 * F * R * J + 2 * R * N * J

F32 = mybir.dt.float32
BF16 = mybir.dt.bfloat16
I32 = mybir.dt.int32
U32 = mybir.dt.uint32
U16 = mybir.dt.uint16
U8 = mybir.dt.uint8
E4M3 = mybir.dt.float8_e4m3fn_x4
E5M2 = mybir.dt.float8_e5m2_x4
E2M1 = mybir.dt.float4_e2m1fn_x4
ALU = mybir.AluOpType
ACT = mybir.ActivationFunctionType

P = 128
PACK = 4
HALF = 128
HALVES = J // HALF
LIST_COLS = HALF // 16
W_AT, W2_AT, XO_AT, WB_AT = 0, R, 2 * R, 2 * R + J
SCALE_COLS = WB_AT + N
ROWS_AT = P - 16


def tile_list_two_largerpicks_other_absgap_residual_kernel(
    tc, xf, fk, w_words, w_scales, xo_words, xo_scales, w2_words, w2_scales, wb_words, wb_scales, rs, gm, offs, offs2, offs3, out
):
    nc = tc.nc
    with ExitStack() as ctx:
        sb = ctx.enter_context(tc.tile_pool(name="sb", bufs=1))
        ps = ctx.enter_context(tc.psum_pool(name="ps", bufs=1))

        list_a = sb.tile([P, J // 16], U16, name="list_a")
        list_b = sb.tile([P, J // 16], U16, name="list_b")
        list_o = sb.tile([P, J // 16], U16, name="list_o")
        x_pair = [sb.tile([P, 2, T], F32, name="x_pair%d" % a) for a in range(2)]
        x_plane = [x_pair[t // 2][:, t % 2, :] for t in range(PACK)]
        fk_sb = sb.tile([P, PACK], F32, name="fk_sb")
        fk_neg = sb.tile([P, PACK], F32, name="fk_neg")
        w_raw = sb.tile([P, R], U16, name="w_raw", tag="w_raw", align_bytes=64)
        w2_raw = sb.tile([P, R], U32, name="w2_raw", tag="w2_raw")
        ws_raw = sb.tile([P, 2 * R], U8, name="ws_raw")
        xo_tab = sb.tile([P, Z], U32, name="xo_tab", tag="xo_tab")
        xo_tab_s = sb.tile([P, Z], U8, name="xo_tab_s")
        rows = sb.tile([P, SCALE_COLS], U8, name="rows", tag="rows")
        planes = sb.tile([P, SCALE_COLS], U8, name="planes", align_bytes=64)
        xo_picked_s = sb.tile([P, J], U8, name="xo_picked_s", tag="after_spread", align_bytes=64)

        warm = sb.tile([P, 2], F32, name="warm")
        nc.gpsimd.memset(warm[:, 0:1], 0.0)
        nc.vector.memset(ws_raw[0:ROWS_AT, :].bitcast(I32), 0)
        nc.vector.memset(xo_tab_s[0:ROWS_AT, :].bitcast(I32), 0)
        nc.vector.memset(planes[:].bitcast(I32), 0)
        x_rows = xf.rearrange("(p t) c -> p t c", t=PACK)
        nc.sync.dma_start(list_o[:], offs3)
        nc.scalar.dma_start(out=xo_tab_s[ROWS_AT:P, :].bitcast(I32), in_=xo_scales[0].bitcast(I32))
        nc.sync.dma_start(list_a[:], offs)
        nc.scalar.dma_start(out=ws_raw[ROWS_AT:P, R : 2 * R].bitcast(I32), in_=w2_scales[0].bitcast(I32))
        nc.scalar.dma_start(out=ws_raw[ROWS_AT:P, 0:R].bitcast(I32), in_=w_scales[0].bitcast(I32))
        nc.sync.dma_start(out=x_pair[0][:], in_=x_rows[:, 0:2, :])
        nc.sync.dma_start(list_b[:], offs2)
        nc.sync.dma_start(out=x_pair[1][:], in_=x_rows[:, 2:4, :])
        nc.scalar.activation(warm[:, 1:2], warm[:, 0:1], ACT.Copy)
        nc.sync.dma_start(out=fk_sb[:], in_=fk.rearrange("(p t) o -> p (t o)", t=PACK))
        nc.gpsimd.tensor_scalar(fk_neg[:], fk_sb[:], -1.0, 0.0, ALU.mult, ALU.add)
        nc.sync.dma_start(out=rows[ROWS_AT:P, WB_AT:SCALE_COLS].bitcast(I32), in_=wb_scales[0].bitcast(I32))
        nc.sync.dma_start(out=xo_tab[:].bitcast(I32), in_=xo_words[0].rearrange("p n t -> p (n t)").bitcast(I32))
        nc.sync.dma_start(out=w2_raw[:].bitcast(I32), in_=w2_words[0].rearrange("p n t -> p (n t)").bitcast(I32))
        nc.sync.dma_start(out=w_raw[:].bitcast(I32), in_=w_words[0].bitcast(I32))

        pick_a = sb.tile([P, PACK, J], F32, name="pick_a")
        pick_b = sb.tile([P, PACK, J], F32, name="pick_b")

        w_c = sb.tile([P, R], U16, name="w_c", align_bytes=64)
        w2_c = sb.tile([P, R], U32, name="w2_c", align_bytes=64)
        xo_c = sb.tile([P, J], U32, name="xo_c", align_bytes=64)
        gap = [ps.tile([P, PACK, HALF], F32, name="gap%d" % h) for h in range(HALVES)]
        prod = [ps.tile([P, N // P, HALF], F32, name="prod%d" % h) for h in range(HALVES)]
        u_c = [sb.tile([P, HALF], U32, name="u_c%d" % h, align_bytes=64) for h in range(HALVES)]
        u_s = [sb.tile([P, HALF], U8, name="u_s%d" % h, align_bytes=64) for h in range(HALVES)]
        hid_bf = [sb.tile([P, HALF * PACK], BF16, name="hid_bf%d" % h, align_bytes=64) for h in range(HALVES)]
        hid_c = [sb.tile([P, HALF], U32, name="hid_c%d" % h, align_bytes=64) for h in range(HALVES)]
        hid_s = [sb.tile([P, HALF], U8, name="hid_s%d" % h, align_bytes=64) for h in range(HALVES)]
        y = [sb.tile([P, N // P, HALF], F32, name="y%d" % h) for h in range(HALVES)]
        out_rows = out.rearrange("(c p) j -> p c j", p=P)

        def pick_scalar(dst, lst, t, lo, hi):
            nc.scalar.activation(dst[:, t, lo:hi], x_plane[t].indirect(lst[:, lo // 16 : hi // 16]), ACT.Copy)

        def pick_vector(dst, lst, t, lo, hi):
            nc.vector.tensor_copy(dst[:, t, lo:hi], x_plane[t].indirect(lst[:, lo // 16 : hi // 16]))

        def keep_larger(larger, h):
            cols = slice(h * HALF, (h + 1) * HALF)
            nc.vector.tensor_tensor(larger[:], pick_a[:, :, cols], pick_b[:, :, cols], ALU.max)

        def deal(dst, src, per_line):
            nc.vector.tensor_copy(
                out=dst.rearrange("p (s t c i) -> p s c t i", t=PACK, c=P // per_line, i=per_line),
                in_=src.rearrange("p (s c i t) -> p s c t i", t=PACK, c=P // per_line, i=per_line),
            )

        def scale_u(u_bf, larger):
            nc.vector.tensor_tensor(
                u_bf[:].rearrange("p (c i t) -> p c t i", i=4, t=PACK),
                larger[:].rearrange("p t (c i) -> p c t i", i=4),
                fk_neg[:].unsqueeze(1).unsqueeze(3).to_broadcast([P, HALF // 4, PACK, 4]),
                ALU.mult,
            )

        def quantize_u(u_bf, h):
            nc.vector.quantize_mx(out=u_c[h][:].bitcast(E4M3), scales=u_s[h][:], in_=u_bf[:])

        def side_passes(h, first):
            cols = slice(h * HALF, (h + 1) * HALF)
            for t in range(PACK):
                nc.tensor.matmul_mx(
                    out=gap[h][:, t, :],
                    lhsT=w2_c[:, t * P : (t + 1) * P].bitcast(E5M2),
                    lhsT_scale=planes[:, W2_AT + t * P : W2_AT + (t + 1) * P],
                    rhs=xo_c[:, cols].bitcast(E4M3),
                    rhs_scale=planes[:, XO_AT + h * HALF : XO_AT + (h + 1) * HALF],
                    start=(first and t == 0),
                    stop=(not first and t == PACK - 1),
                )

        def token_passes(h, first):
            for t in range(PACK):
                nc.tensor.matmul_mx(
                    out=gap[h][:, t, :],
                    lhsT=w_c[:, t * P : (t + 1) * P].bitcast(E2M1),
                    lhsT_scale=planes[:, W_AT + t * P : W_AT + (t + 1) * P],
                    rhs=u_c[h][:].bitcast(E4M3),
                    rhs_scale=u_s[h][:],
                    start=(first and t == 0),
                    stop=(not first and t == PACK - 1),
                )

        def magnitude(h):
            nc.scalar.activation(
                hid_bf[h][:].rearrange("p (j t) -> p j t", t=PACK), gap[h][:].rearrange("p t j -> p j t"), ACT.Abs
            )

        def second_stage(h):
            nc.vector.quantize_mx(out=hid_c[h][:].bitcast(E5M2), scales=hid_s[h][:], in_=hid_bf[h][:])
            for c in range(N // P):
                nc.tensor.matmul_mx(
                    out=prod[h][:, c, :],
                    lhsT=wb_c[:, c * P : (c + 1) * P].bitcast(E5M2),
                    lhsT_scale=planes[:, WB_AT + c * P : WB_AT + (c + 1) * P],
                    rhs=hid_c[h][:].bitcast(E5M2),
                    rhs_scale=hid_s[h][:],
                    start=True,
                    stop=True,
                )

        def finish(h):
            cols = slice(h * HALF, (h + 1) * HALF)
            for c in range(N // P):
                nc.vector.scalar_tensor_tensor(
                    y[h][:, c, :], prod[h][:, c, :], gm_sb[:, c : c + 1], rs_sb[:, c, cols], ALU.mult, ALU.add
                )
                nc.sync.dma_start(out=out_rows[:, c, cols], in_=y[h][:, c, :])

        nc.vector.tensor_copy(xo_picked_s[:], xo_tab_s[:].indirect(list_o[:]))
        deal(rows[:, W_AT:XO_AT], ws_raw[:], 16)
        nc.vector.tensor_copy(rows[:, XO_AT : XO_AT + J].bitcast(I32), xo_picked_s[:].bitcast(I32))
        for quad in range(4):
            nc.sync.dma_start(
                out=planes[32 * quad : 32 * quad + 4, :].bitcast(I32), in_=rows[ROWS_AT + 4 * quad : ROWS_AT + 4 * quad + 4, :].bitcast(I32)
            )
        wb_c = sb.tile([P, N], U32, name="wb_c", tag="after_spread", align_bytes=64)
        nc.sync.dma_start(out=wb_c[:].bitcast(I32), in_=wb_words[0].rearrange("p n t -> p (n t)").bitcast(I32))
        pick_scalar(pick_a, list_a, 0, 0, J)
        pick_vector(pick_b, list_b, 0, 0, J)
        pick_scalar(pick_a, list_a, 1, 0, J)
        pick_vector(pick_b, list_b, 1, 0, J)
        for h in range(HALVES):
            for t in range(2, PACK):
                pick_scalar(pick_a, list_a, t, h * HALF, (h + 1) * HALF)
                pick_scalar(pick_b, list_b, t, h * HALF, (h + 1) * HALF)
        late = sb.tile([P, (N // P) * (J + 1)], F32, name="late", tag="rows")
        rs_sb = late[:, 0 : (N // P) * J].rearrange("p (c j) -> p c j", j=J)
        gm_sb = late[:, (N // P) * J :]
        nc.sync.dma_start(out=rs_sb, in_=rs.rearrange("(c p) j -> p c j", p=P))
        with nc.allow_non_contiguous_dma(reason="one factor a partition and output tile"):
            nc.sync.dma_start(out=gm_sb, in_=gm.rearrange("(c p) o -> p (c o)", p=P))
        nc.vector.tensor_copy(xo_c[:], xo_tab[:].indirect(list_o[:]))
        larger0 = sb.tile([P, PACK, HALF], F32, name="larger0", tag="xo_tab")
        u_bf0 = sb.tile([P, HALF * PACK], BF16, name="u_bf0", align_bytes=64)
        keep_larger(larger0, 0)
        deal(w2_c[:], w2_raw[:], 4)
        side_passes(0, True)
        side_passes(1, True)
        scale_u(u_bf0, larger0)
        deal(w_c[:], w_raw[:], 8)
        quantize_u(u_bf0, 0)
        token_passes(0, False)
        magnitude(0)
        larger1 = sb.tile([P, PACK, HALF], F32, name="larger1", tag="w2_raw")
        u_bf1 = sb.tile([P, HALF * PACK], BF16, name="u_bf1", tag="w_raw", align_bytes=64)
        keep_larger(larger1, 1)
        scale_u(u_bf1, larger1)
        quantize_u(u_bf1, 1)
        token_passes(1, False)
        second_stage(0)
        magnitude(1)
        second_stage(1)
        finish(0)
        finish(1)
